import numpy as np
import ml_dtypes


def mxq(x, axis, fmt="e4m3"):
    dtype, down = {"e4m3": (ml_dtypes.float8_e4m3fn, 7), "e5m2": (ml_dtypes.float8_e5m2, 14)}[fmt]
    v = np.moveaxis(np.asarray(x, np.float32).astype(ml_dtypes.bfloat16).astype(np.float64), axis, -1)
    blocks = v.reshape(v.shape[:-1] + (-1, 32))
    amax = np.abs(blocks).max(-1, keepdims=True)
    byte = np.maximum(np.where(amax > 0, np.frexp(amax)[1] - 1 + 127, 0) - down, 1)
    scale = np.exp2(byte - 127.0)
    codes = (blocks / scale).astype(np.float32).astype(dtype).astype(np.float64)
    return np.moveaxis((codes * scale).reshape(v.shape), -1, axis)


WIDE = False


def mx_kscale(k):
    if not WIDE:
        return np.ones(k)
    levels = np.array([10, -10, 5, -5, 0])
    if k % 512:
        return np.exp2(np.random.permutation(np.resize(levels, k // 32))).repeat(32)
    a = np.empty((k // 512, 16))
    for p in range(k // 512):
        a[p, :8] = np.random.permutation(np.resize(levels, 8))
        for g in range(8):
            far = levels[np.abs(levels - a[p, g]) >= 10]
            a[p, g + 8] = far[np.random.randint(len(far))]
    return np.exp2(a.ravel()).repeat(32)


def f64(x):
    return np.asarray(x).astype(np.float64)


def striped(idx):
    return np.tile(idx.reshape(-1, 16).T, (8, 1)).astype(np.uint16)


def unstriped(offs):
    return offs[:16].T.reshape(-1).astype(np.int64)


def pack_weight(w):
    k, n = w.shape
    w = f64(np.asarray(w, np.float32).astype(ml_dtypes.bfloat16)).reshape(k // 32, 32, n)
    amax = np.abs(w).max(1)
    byte = np.clip(np.where(amax > 0, np.frexp(amax)[1] - 1 + 127 - 7, 1), 1, 254)
    scaled = (w * np.exp2(127.0 - byte)[:, None, :]).reshape(k, n).astype(np.float32)
    words = np.ascontiguousarray(scaled.reshape(k // 512, 128, 4, n).transpose(0, 1, 3, 2)).astype(ml_dtypes.float8_e4m3fn).view(np.uint8)
    return words, np.ascontiguousarray(byte.astype(np.uint8).reshape(k // 512, 16, n))


def unpack_weight(words, scales):
    g, p, n, _ = words.shape
    vals = np.ascontiguousarray(words).view(ml_dtypes.float8_e4m3fn).astype(np.float64) * np.repeat(np.exp2(scales.astype(np.float64) - 127.0), 8, axis=1)[..., None]
    return vals.transpose(0, 1, 3, 2).reshape(g * 512, n)


K, T, S, N, U = 1024, 1024, 512, 256, 512
P = 2 ** 7


def setup_inputs():
    n = np.random.standard_normal
    s = mx_kscale(K)[:, None]
    packed_xT = pack_weight(n((K, T)) * s)
    return {
        "x_words": packed_xT[0],
        "x_scales": packed_xT[1],
        "w1": (n((K, N)) / np.sqrt(K) / s).astype(np.float32),
        "w2": (n((K, N)) / np.sqrt(K) / s).astype(np.float32),
        "w3": (n((K, N)) / np.sqrt(K) / s).astype(np.float32),
        "chg": (np.tile(np.random.uniform(0.3, 1.0, S) * np.where(np.random.uniform(size=S) < 0.5, 1.0, -1.0), (P, 1))).astype(np.float32),
        "offs": striped(np.random.permutation(T)[:S]),
        "ia": striped(np.random.randint(0, S, U)),
        "ib": striped(np.random.randint(0, S, U)),
    }


def reference(x_words, x_scales, w1, w2, w3, chg, offs, ia, ib):
    xq = unpack_weight(x_words, x_scales)[:, unstriped(offs)]
    y = mxq(f64(w1), 0, "e4m3").T @ xq
    dx = y[:, unstriped(ia)] - y[:, unstriped(ib)]
    z = mxq(f64(w2), 0, "e4m3").T @ xq
    dy = z[:, unstriped(ia)] - z[:, unstriped(ib)]
    rsq = (dx) ** 2 + (dy) ** 2 + 0.1
    yr = mxq(f64(w3), 0, "e4m3").T @ xq
    born = np.log(np.exp(yr) + 1.0) + 0.4
    ab = born[:, unstriped(ia)] * born[:, unstriped(ib)]
    ex = np.exp(-0.25 * (rsq / ab))
    fsq = rsq + ab * ex
    en = ((f64(chg)[:1][:, unstriped(ia)]) * (f64(chg)[:1][:, unstriped(ib)])) / np.sqrt(fsq)
    return ((en * (-1.0 * (0.25 * ex) + 1.0)) * dx) / fsq

@@ -1,0 +1,189 @@
+from contextlib import ExitStack
+
+import concourse.mybir as mybir
+
+K, T, S, N, U = 1024, 1024, 512, 256, 512
+FLOPS = 3 * 2 * K * N * S
+
+F32 = mybir.dt.float32
+BF16 = mybir.dt.bfloat16
+I32 = mybir.dt.int32
+U32 = mybir.dt.uint32
+U16 = mybir.dt.uint16
+U8 = mybir.dt.uint8
+FP8X4 = mybir.dt.float8_e4m3fn_x4
+ALU = mybir.AluOpType
+ACT = mybir.ActivationFunctionType
+
+P = 128
+PACK = 4
+K_PASS = P * PACK
+PASSES = K // K_PASS
+BLOCKS = N // P
+VECTOR_WINDOW = 1024
+SCALAR_WINDOW = 2048
+CHARGE_WINDOW = 704
+LN_FLOOR = 1e-19
+
+
+def tile_picked_ygborn_force_p_kernel(
+    tc, x_words, x_scales, w1, w2, w3, chg, offs, ia, ib, out
+):
+    nc = tc.nc
+    with ExitStack() as ctx:
+        keep = ctx.enter_context(tc.tile_pool(name="keep", bufs=1))
+        psum = ctx.enter_context(tc.psum_pool(name="psum", bufs=1))
+
+        def tile(name, shape, dtype=F32):
+            return keep.tile(shape, dtype, name=name, align_bytes=64)
+
+        picked = tile("picked", [P, S // 16], U16)
+        first = tile("first", [P, U // 16], U16)
+        second = tile("second", [P, U // 16], U16)
+        words = [tile(f"words{o}", [P, T], U32) for o in range(PASSES)]
+        scales = tile("scales", [P, T], U8)
+        charge = tile("charge", [P, CHARGE_WINDOW])
+        y_win = [tile(f"y{b}", [P, VECTOR_WINDOW]) for b in range(BLOCKS)]
+        z_win = [tile(f"z{b}", [P, VECTOR_WINDOW]) for b in range(BLOCKS)]
+        lnb_win = [tile(f"lnb{b}", [P, SCALAR_WINDOW]) for b in range(BLOCKS)]
+        weights = {"r": w3, "y": w1, "z": w2}
+        raw = {(m, o): tile(f"raw_{m}{o}", [P, PACK, N]) for m in weights for o in range(PASSES)}
+        sig = lnb_win[0][:, S : 3 * S]
+        ln_sig = lnb_win[1][:, S : 3 * S]
+        soft = [lnb_win[b][:, 3 * S :] for b in range(BLOCKS)]
+
+        nc.gpsimd.memset(scales[:].bitcast(I32), 0)
+        nc.vector.memset(charge[:, S:], 0.0)
+        for win in y_win + z_win:
+            nc.vector.memset(win[:, S:], 0.0)
+
+        def load_weights(m, o):
+            rows = weights[m][o * K_PASS : (o + 1) * K_PASS, :]
+            nc.sync.dma_start(out=raw[m, o][:], in_=rows.rearrange("(p j) n -> p j n", j=PACK))
+
+        def load_words(o):
+            nc.sync.dma_start(
+                out=words[o][:].bitcast(I32),
+                in_=x_words[o].rearrange("p n t -> p (n t)").bitcast(I32),
+            )
+
+        nc.sync.dma_start(out=picked[:], in_=offs)
+        load_words(0)
+        for q in range(4):
+            nc.sync.dma_start(
+                out=scales[32 * q : 32 * q + 4 * PASSES, :].bitcast(I32),
+                in_=x_scales[:, 4 * q : 4 * q + 4, :].bitcast(I32),
+            )
+        load_weights("r", 0)
+        load_words(1)
+        load_weights("r", 1)
+        nc.sync.dma_start(out=first[:], in_=ia)
+        nc.sync.dma_start(out=second[:], in_=ib)
+        nc.sync.dma_start(out=charge[:, :S], in_=chg)
+        for m in ("y", "z"):
+            for o in range(PASSES):
+                load_weights(m, o)
+
+        x_codes = [tile(f"x_codes{o}", [P, S], U32) for o in range(PASSES)]
+        x_bytes = tile("x_bytes", [P, S], U8)
+        q_first = tile("q_first", [P, U])
+        q_pair = tile("q_pair", [P, U])
+        nc.vector.tensor_copy(x_codes[0][:], words[0][:].indirect(picked[:]))
+        nc.vector.tensor_copy(x_bytes[:], scales[:].indirect(picked[:]))
+        nc.vector.tensor_copy(x_codes[1][:], words[1][:].indirect(picked[:]))
+
+        acc = {(m, b): psum.tile([P, S], F32, name=f"acc_{m}{b}") for m in weights for b in range(BLOCKS)}
+
+        def product(m, engines):
+            quantised = []
+            for o in range(PASSES):
+                grouped = tile(f"grouped_{m}{o}", [P, N, PACK], BF16)
+                dst = grouped[:].rearrange("p (c i) t -> p c t i", i=4)
+                src = raw[m, o][:].rearrange("p t (c i) -> p c t i", i=4)
+                if engines[o] == "S":
+                    nc.scalar.copy(dst, src)
+                elif engines[o] == "V":
+                    nc.vector.tensor_copy(dst, src)
+                else:
+                    nc.gpsimd.tensor_scalar(
+                        grouped[:], raw[m, o][:].rearrange("p t n -> p n t"), 1.0, 0.0, ALU.mult, ALU.add
+                    )
+                codes = tile(f"codes_{m}{o}", [P, N], U32)
+                plane = tile(f"plane_{m}{o}", [P, N], U8)
+                nc.vector.quantize_mx(
+                    out=codes[:].bitcast(FP8X4), scales=plane[:], in_=grouped[:].rearrange("p n t -> p (n t)")
+                )
+                quantised.append((codes, plane))
+            for b in range(BLOCKS):
+                cols = slice(b * P, (b + 1) * P)
+                for o, (codes, plane) in enumerate(quantised):
+                    nc.tensor.matmul_mx(
+                        out=acc[m, b][:],
+                        lhsT=codes[:, cols].bitcast(FP8X4),
+                        lhsT_scale=plane[:, cols],
+                        rhs=x_codes[o][:].bitcast(FP8X4),
+                        rhs_scale=x_bytes[4 * o :, :],
+                        start=(o == 0),
+                        stop=(o == PASSES - 1),
+                    )
+
+        def pairs(name):
+            return [tile(f"{name}{b}", [P, U])[:] for b in range(BLOCKS)]
+
+        y_second, dx, z_second, dy = pairs("y_second"), pairs("dx"), pairs("z_second"), pairs("dy")
+        dx2, dy2, rsq, dxq = pairs("dx2"), pairs("dy2"), pairs("rsq"), pairs("dxq")
+        h_first, h_second, c, inv = pairs("h_first"), pairs("h_second"), pairs("c"), pairs("inv")
+        s, ex, g, g2, g3, c3, tq, a, res = (pairs(n) for n in ("s", "ex", "g", "gsq", "gcube", "ccube", "tq", "a", "res"))
+        rg = [s[1], s[0]]
+
+        product("r", "SS")
+        for b in range(BLOCKS):
+            nc.scalar.activation(sig[:, b * S : (b + 1) * S], acc["r", b][:], ACT.Sigmoid, scale=-1.0)
+        nc.scalar.activation(ln_sig, sig, ACT.Ln, bias=LN_FLOOR)
+        for b in range(BLOCKS):
+            nc.vector.scalar_tensor_tensor(
+                soft[b], ln_sig[:, b * S : (b + 1) * S], -1.0, acc["r", b][:], ALU.mult, ALU.max
+            )
+        for b in range(BLOCKS):
+            nc.scalar.activation(lnb_win[b][:, :S], soft[b], ACT.Ln, bias=0.4)
+        product("y", "SV")
+        for b in range(BLOCKS):
+            nc.scalar.copy(y_win[b][:, :S], acc["y", b][:])
+        product("z", "VV")
+        for b in range(BLOCKS):
+            nc.scalar.copy(z_win[b][:, :S], acc["z", b][:])
+        nc.vector.tensor_copy(q_first[:], charge[:].indirect(first[:]))
+        nc.vector.tensor_tensor(q_pair[:], charge[:].indirect(second[:]), q_first[:], ALU.mult)
+
+        for b in range(BLOCKS):
+            nc.scalar.activation(h_first[b], lnb_win[b][:].indirect(first[:]), ACT.Exp, scale=-0.5)
+            nc.scalar.activation(h_second[b], lnb_win[b][:].indirect(second[:]), ACT.Exp, scale=-0.5)
+            nc.vector.tensor_tensor(c[b], h_first[b], h_second[b], ALU.mult)
+            nc.scalar.activation(inv[b], c[b], ACT.Square)
+        for b in range(BLOCKS):
+            nc.vector.tensor_copy(y_second[b], y_win[b][:].indirect(second[:]))
+            nc.vector.tensor_tensor(dx[b], y_win[b][:].indirect(first[:]), y_second[b], ALU.subtract)
+            nc.scalar.activation(dx2[b], dx[b], ACT.Square)
+            nc.vector.tensor_copy(z_second[b], z_win[b][:].indirect(second[:]))
+            nc.vector.tensor_tensor(dy[b], z_win[b][:].indirect(first[:]), z_second[b], ALU.subtract)
+            nc.scalar.activation(dy2[b], dy[b], ACT.Square)
+        for b in range(BLOCKS):
+            nc.vector.scalar_tensor_tensor(rsq[b], dx2[b], 0.1, dy2[b], ALU.add, ALU.add)
+            nc.vector.tensor_tensor(s[b], rsq[b], inv[b], ALU.mult)
+            nc.scalar.activation(ex[b], s[b], ACT.Exp, scale=-0.25)
+        for b in range(BLOCKS):
+            nc.vector.tensor_tensor(g[b], s[b], ex[b], ALU.add)
+            if b == 0:
+                nc.scalar.activation(g2[b], g[b], ACT.Square)
+            else:
+                nc.vector.tensor_tensor(g2[b], g[b], g[b], ALU.mult)
+            nc.vector.tensor_tensor(g3[b], g2[b], g[b], ALU.mult)
+        for b in range(BLOCKS):
+            nc.scalar.activation(rg[b], g3[b], ACT.Abs_reciprocal_sqrt)
+        for b in range(BLOCKS):
+            nc.vector.scalar_tensor_tensor(dxq[b], dx[b], -0.25, q_pair[:], ALU.mult, ALU.mult)
+            nc.vector.tensor_tensor(c3[b], c[b], inv[b], ALU.mult)
+            nc.vector.tensor_tensor(tq[b], dxq[b], c3[b], ALU.mult)
+            nc.vector.scalar_tensor_tensor(a[b], ex[b], -4.0, tq[b], ALU.add, ALU.mult)
+            nc.vector.tensor_tensor(res[b], a[b], rg[b], ALU.mult)
+            nc.sync.dma_start(out=out[b * P : (b + 1) * P, :], in_=res[b])

@@ -1,6 +1,7 @@
 from contextlib import ExitStack
 
 import concourse.mybir as mybir
+from concourse.masks import make_identity
 
 K, T, S, N, U = 1024, 1024, 512, 256, 512
 FLOPS = 3 * 2 * K * N * S
@@ -49,13 +50,16 @@ def tile_picked_ygborn_force_p_kernel(
         weights = {"r": w3, "y": w1, "z": w2}
         raw = {(m, o): tile(f"raw_{m}{o}", [P, PACK, N]) for m in weights for o in range(PASSES)}
         sig = lnb_win[0][:, S : 3 * S]
-        ln_sig = lnb_win[1][:, S : 3 * S]
-        soft = [lnb_win[b][:, 3 * S :] for b in range(BLOCKS)]
+        ln_sig = tile("ln_sig", [P, BLOCKS * S])[:]
+        ident = tile("ident", [P, P])
 
         nc.gpsimd.memset(scales[:].bitcast(I32), 0)
         nc.vector.memset(charge[:, S:], 0.0)
         for win in y_win + z_win:
             nc.vector.memset(win[:, S:], 0.0)
+        make_identity(nc, ident[:])
+        warm = tile("warm", [P, 1])
+        nc.scalar.activation(warm[:], charge[:, S : S + 1], ACT.Sigmoid)
 
         def load_weights(m, o):
             rows = weights[m][o * K_PASS : (o + 1) * K_PASS, :]
@@ -77,50 +81,55 @@ def tile_picked_ygborn_force_p_kernel(
         load_weights("r", 0)
         load_words(1)
         load_weights("r", 1)
+        load_weights("y", 0)
+        load_weights("y", 1)
         nc.sync.dma_start(out=first[:], in_=ia)
         nc.sync.dma_start(out=second[:], in_=ib)
         nc.sync.dma_start(out=charge[:, :S], in_=chg)
-        for m in ("y", "z"):
-            for o in range(PASSES):
-                load_weights(m, o)
+        load_weights("z", 0)
+        load_weights("z", 1)
 
         x_codes = [tile(f"x_codes{o}", [P, S], U32) for o in range(PASSES)]
         x_bytes = tile("x_bytes", [P, S], U8)
-        q_first = tile("q_first", [P, U])
-        q_pair = tile("q_pair", [P, U])
+        q_first = tile("q_first", [P, U])[:]
+        q_pair = tile("q_pair", [P, U])[:]
         nc.vector.tensor_copy(x_codes[0][:], words[0][:].indirect(picked[:]))
         nc.vector.tensor_copy(x_bytes[:], scales[:].indirect(picked[:]))
         nc.vector.tensor_copy(x_codes[1][:], words[1][:].indirect(picked[:]))
 
-        acc = {(m, b): psum.tile([P, S], F32, name=f"acc_{m}{b}") for m in weights for b in range(BLOCKS)}
+        acc = {(m, b): psum.tile([P, S], F32, name=f"acc_{m}{b}", tag=f"{m}{b}") for m in weights for b in range(BLOCKS)}
 
-        def product(m, engines):
-            quantised = []
-            for o in range(PASSES):
-                grouped = tile(f"grouped_{m}{o}", [P, N, PACK], BF16)
-                dst = grouped[:].rearrange("p (c i) t -> p c t i", i=4)
-                src = raw[m, o][:].rearrange("p t (c i) -> p c t i", i=4)
-                if engines[o] == "S":
-                    nc.scalar.copy(dst, src)
-                elif engines[o] == "V":
-                    nc.vector.tensor_copy(dst, src)
-                else:
-                    nc.gpsimd.tensor_scalar(
-                        grouped[:], raw[m, o][:].rearrange("p t n -> p n t"), 1.0, 0.0, ALU.mult, ALU.add
-                    )
-                codes = tile(f"codes_{m}{o}", [P, N], U32)
-                plane = tile(f"plane_{m}{o}", [P, N], U8)
-                nc.vector.quantize_mx(
-                    out=codes[:].bitcast(FP8X4), scales=plane[:], in_=grouped[:].rearrange("p n t -> p (n t)")
+        grouped = {key: tile(f"grouped_{key[0]}{key[1]}", [P, N * PACK], BF16)[:] for key in raw}
+        for o in (0, 1):
+            grouped["z", o] = ln_sig[:, o * S : (o + 1) * S].bitcast(BF16)
+        codes = {key: tile(f"codes_{key[0]}{key[1]}", [P, N], U32) for key in raw}
+        plane = {key: tile(f"plane_{key[0]}{key[1]}", [P, N], U8) for key in raw}
+
+        def quantise(m, o, engine, lo=0, hi=N):
+            dst = grouped[m, o][:, lo * PACK : hi * PACK].rearrange("p (c i t) -> p c t i", i=4, t=PACK)
+            src = raw[m, o][:, :, lo:hi].rearrange("p t (c i) -> p c t i", i=4)
+            if engine == "S":
+                nc.scalar.copy(dst, src)
+            elif engine == "V":
+                nc.vector.tensor_copy(dst, src)
+            else:
+                nc.gpsimd.tensor_scalar(
+                    grouped[m, o].rearrange("p (n t) -> p n t", t=PACK), raw[m, o][:].rearrange("p t n -> p n t"), 1.0, 0.0, ALU.mult, ALU.add
                 )
-                quantised.append((codes, plane))
+            nc.vector.quantize_mx(
+                out=codes[m, o][:, lo:hi].bitcast(FP8X4),
+                scales=plane[m, o][:, lo:hi],
+                in_=grouped[m, o][:, lo * PACK : hi * PACK],
+            )
+
+        def product(m):
             for b in range(BLOCKS):
                 cols = slice(b * P, (b + 1) * P)
-                for o, (codes, plane) in enumerate(quantised):
+                for o in range(PASSES):
                     nc.tensor.matmul_mx(
                         out=acc[m, b][:],
-                        lhsT=codes[:, cols].bitcast(FP8X4),
-                        lhsT_scale=plane[:, cols],
+                        lhsT=codes[m, o][:, cols].bitcast(FP8X4),
+                        lhsT_scale=plane[m, o][:, cols],
                         rhs=x_codes[o][:].bitcast(FP8X4),
                         rhs_scale=x_bytes[4 * o :, :],
                         start=(o == 0),
@@ -130,13 +139,34 @@ def tile_picked_ygborn_force_p_kernel(
         def pairs(name):
             return [tile(f"{name}{b}", [P, U])[:] for b in range(BLOCKS)]
 
-        y_second, dx, z_second, dy = pairs("y_second"), pairs("dx"), pairs("z_second"), pairs("dy")
-        dx2, dy2, rsq, dxq = pairs("dx2"), pairs("dy2"), pairs("rsq"), pairs("dxq")
-        h_first, h_second, c, inv = pairs("h_first"), pairs("h_second"), pairs("c"), pairs("inv")
-        s, ex, g, g2, g3, c3, tq, a, res = (pairs(n) for n in ("s", "ex", "g", "gsq", "gcube", "ccube", "tq", "a", "res"))
-        rg = [s[1], s[0]]
+        def turn(bank, terms, lo=0, hi=U):
+            for j in range(lo // P, hi // P):
+                cols = slice(j * P, (j + 1) * P)
+                for n, term in enumerate(terms):
+                    nc.tensor.matmul(
+                        bank[:, cols], term[:, cols], ident[:], is_transpose=True,
+                        start=(n == 0), stop=(n == len(terms) - 1),
+                    )
 
-        product("r", "SS")
+        def bank(name, tag):
+            return psum.tile([P, U], F32, name=name, tag=tag)[:]
+
+        y_second, dx, z_second, dy = pairs("y_second"), pairs("dx"), pairs("z_second"), pairs("dy")
+        dx2, dy2 = pairs("dx2"), pairs("dy2")
+        soft = [lnb_win[b][:, 3 * S :] for b in range(BLOCKS)]
+        lnb = [lnb_win[1][:, (1 + b) * S : (2 + b) * S] for b in range(BLOCKS)]
+        h_first, h_second, inv, c3 = pairs("h_first"), pairs("h_second"), pairs("inv"), pairs("ccube")
+        s, ex, g2, g3, tq, a, res = (pairs(n) for n in ("s", "ex", "gsq", "gcube", "tq", "a", "res"))
+        rg = [s[1], s[0]]
+        q_col = tile("q_col", [P, U // P])
+
+        quantise("r", 0, "S")
+        quantise("r", 1, "V", 0, P)
+        quantise("r", 1, "S", P, N)
+        product("r")
+        quantise("y", 0, "V")
+        quantise("y", 1, "V")
+        product("y")
         for b in range(BLOCKS):
             nc.scalar.activation(sig[:, b * S : (b + 1) * S], acc["r", b][:], ACT.Sigmoid, scale=-1.0)
         nc.scalar.activation(ln_sig, sig, ACT.Ln, bias=LN_FLOOR)
@@ -145,45 +175,67 @@ def tile_picked_ygborn_force_p_kernel(
                 soft[b], ln_sig[:, b * S : (b + 1) * S], -1.0, acc["r", b][:], ALU.mult, ALU.max
             )
         for b in range(BLOCKS):
-            nc.scalar.activation(lnb_win[b][:, :S], soft[b], ACT.Ln, bias=0.4)
-        product("y", "SV")
+            nc.scalar.activation(lnb[b], soft[b], ACT.Ln, bias=0.4)
+        for b in range(BLOCKS):
+            nc.scalar.activation(lnb_win[b][:, :S], lnb[b], ACT.Ln, bias=1.0)
         for b in range(BLOCKS):
             nc.scalar.copy(y_win[b][:, :S], acc["y", b][:])
-        product("z", "VV")
+        quantise("z", 0, "V")
+        quantise("z", 1, "V")
+        product("z")
         for b in range(BLOCKS):
             nc.scalar.copy(z_win[b][:, :S], acc["z", b][:])
-        nc.vector.tensor_copy(q_first[:], charge[:].indirect(first[:]))
-        nc.vector.tensor_tensor(q_pair[:], charge[:].indirect(second[:]), q_first[:], ALU.mult)
-
-        for b in range(BLOCKS):
-            nc.scalar.activation(h_first[b], lnb_win[b][:].indirect(first[:]), ACT.Exp, scale=-0.5)
-            nc.scalar.activation(h_second[b], lnb_win[b][:].indirect(second[:]), ACT.Exp, scale=-0.5)
-            nc.vector.tensor_tensor(c[b], h_first[b], h_second[b], ALU.mult)
-            nc.scalar.activation(inv[b], c[b], ACT.Square)
+        pieces = [(0, 0, U), (1, 0, U // 2), (1, U // 2, U)]
+        tail = [(0, 0, U), (1, 0, U // 2), (1, U // 2, U)]
         for b in range(BLOCKS):
             nc.vector.tensor_copy(y_second[b], y_win[b][:].indirect(second[:]))
             nc.vector.tensor_tensor(dx[b], y_win[b][:].indirect(first[:]), y_second[b], ALU.subtract)
-            nc.scalar.activation(dx2[b], dx[b], ACT.Square)
+        for b in range(BLOCKS):
             nc.vector.tensor_copy(z_second[b], z_win[b][:].indirect(second[:]))
-            nc.vector.tensor_tensor(dy[b], z_win[b][:].indirect(first[:]), z_second[b], ALU.subtract)
-            nc.scalar.activation(dy2[b], dy[b], ACT.Square)
+            for c, lo, hi in pieces:
+                if c == b:
+                    nc.vector.tensor_tensor(
+                        dy[b][:, lo:hi], z_win[b][:].indirect(first[:, lo // 16 : hi // 16]), z_second[b][:, lo:hi], ALU.subtract
+                    )
+        nc.vector.tensor_copy(q_first, charge[:].indirect(first[:]))
+        nc.vector.tensor_tensor(q_pair, charge[:].indirect(second[:]), q_first, ALU.mult)
+        ln_ab = [bank(f"ln_ab{b}", f"r{b}") for b in range(BLOCKS)]
         for b in range(BLOCKS):
-            nc.vector.scalar_tensor_tensor(rsq[b], dx2[b], 0.1, dy2[b], ALU.add, ALU.add)
-            nc.vector.tensor_tensor(s[b], rsq[b], inv[b], ALU.mult)
-            nc.scalar.activation(ex[b], s[b], ACT.Exp, scale=-0.25)
+            nc.scalar.activation(h_first[b], lnb_win[b][:].indirect(first[:]), ACT.Exp)
+            nc.scalar.activation(h_second[b], lnb_win[b][:].indirect(second[:]), ACT.Exp)
+            turn(ln_ab[b], (h_first[b], h_second[b]))
         for b in range(BLOCKS):
-            nc.vector.tensor_tensor(g[b], s[b], ex[b], ALU.add)
-            if b == 0:
-                nc.scalar.activation(g2[b], g[b], ACT.Square)
-            else:
-                nc.vector.tensor_tensor(g2[b], g[b], g[b], ALU.mult)
-            nc.vector.tensor_tensor(g3[b], g2[b], g[b], ALU.mult)
+            nc.scalar.activation(dx2[b][:, :], dx[b][:, :], ACT.Square)
+            nc.scalar.activation(inv[b], ln_ab[b], ACT.Exp, scale=-1.0, bias=2.0)
+        for n, (b, lo, hi) in enumerate(pieces):
+            nc.scalar.activation(dy2[b][:, lo:hi], dy[b][:, lo:hi], ACT.Square)
+            rsq = bank(f"rsq{n}", ("x0", "x1", "z1")[n])
+            turn(rsq, (dx2[b], dy2[b]), lo, hi)
+            nc.vector.scalar_tensor_tensor(s[b][:, lo:hi], rsq[:, lo:hi], 0.1, inv[b][:, lo:hi], ALU.add, ALU.mult)
+        for b, lo, hi in pieces:
+            nc.scalar.activation(ex[b][:, lo:hi], s[b][:, lo:hi], ACT.Exp, scale=-0.25)
+        q_turned = bank("q_turned", "z0")
+        turn(q_turned, (q_pair,))
+        nc.vector.tensor_scalar(q_col[:], q_turned[:, 0:U:P], -0.25, None, ALU.mult)
+        dx_turned = [bank(f"dx_turned{b}", f"y{b}") for b in range(BLOCKS)]
         for b in range(BLOCKS):
-            nc.scalar.activation(rg[b], g3[b], ACT.Abs_reciprocal_sqrt)
+            turn(dx_turned[b], (dx[b],))
+            nc.scalar.activation(c3[b], ln_ab[b], ACT.Exp, scale=-1.5, bias=3.0)
+        g = [bank(f"g{b}", f"x{b}") for b in range(BLOCKS)]
+        for b, lo, hi in pieces:
+            turn(g[b], (s[b], ex[b]), lo, hi)
+        a_back = [bank(f"a_back{b}", f"z{b}") for b in range(BLOCKS)]
         for b in range(BLOCKS):
-            nc.vector.scalar_tensor_tensor(dxq[b], dx[b], -0.25, q_pair[:], ALU.mult, ALU.mult)
-            nc.vector.tensor_tensor(c3[b], c[b], inv[b], ALU.mult)
-            nc.vector.tensor_tensor(tq[b], dxq[b], c3[b], ALU.mult)
+            for j in range(U // P):
+                cols = slice(j * P, (j + 1) * P)
+                nc.vector.scalar_tensor_tensor(
+                    tq[b][:, cols], dx_turned[b][:, cols], q_col[:, j : j + 1], c3[b][:, cols], ALU.mult, ALU.mult
+                )
             nc.vector.scalar_tensor_tensor(a[b], ex[b], -4.0, tq[b], ALU.add, ALU.mult)
-            nc.vector.tensor_tensor(res[b], a[b], rg[b], ALU.mult)
-            nc.sync.dma_start(out=out[b * P : (b + 1) * P, :], in_=res[b])
+            turn(a_back[b], (a[b],))
+        for b, lo, hi in tail:
+            nc.scalar.activation(rg[b][:, lo:hi], g[b][:, lo:hi], ACT.Abs_reciprocal_sqrt)
+            nc.scalar.activation(g2[b][:, lo:hi], rg[b][:, lo:hi], ACT.Square)
+            nc.vector.tensor_tensor(g3[b][:, lo:hi], a_back[b][:, lo:hi], rg[b][:, lo:hi], ALU.mult)
+            nc.vector.tensor_tensor(res[b][:, lo:hi], g3[b][:, lo:hi], g2[b][:, lo:hi], ALU.mult)
+            nc.sync.dma_start(out=out[b * P : (b + 1) * P, lo:hi], in_=res[b][:, lo:hi])

@@ -58,8 +58,6 @@ def tile_picked_ygborn_force_p_kernel(
         for win in y_win + z_win:
             nc.vector.memset(win[:, S:], 0.0)
         make_identity(nc, ident[:])
-        warm = tile("warm", [P, 1])
-        nc.scalar.activation(warm[:], charge[:, S : S + 1], ACT.Sigmoid)
 
         def load_weights(m, o):
             rows = weights[m][o * K_PASS : (o + 1) * K_PASS, :]
@@ -100,7 +98,7 @@ def tile_picked_ygborn_force_p_kernel(
         acc = {(m, b): psum.tile([P, S], F32, name=f"acc_{m}{b}", tag=f"{m}{b}") for m in weights for b in range(BLOCKS)}
 
         grouped = {key: tile(f"grouped_{key[0]}{key[1]}", [P, N * PACK], BF16)[:] for key in raw}
-        for o in (0, 1):
+        for o in (1,):
             grouped["z", o] = ln_sig[:, o * S : (o + 1) * S].bitcast(BF16)
         codes = {key: tile(f"codes_{key[0]}{key[1]}", [P, N], U32) for key in raw}
         plane = {key: tile(f"plane_{key[0]}{key[1]}", [P, N], U8) for key in raw}
@@ -158,8 +156,9 @@ def tile_picked_ygborn_force_p_kernel(
         h_first, h_second, inv, c3 = pairs("h_first"), pairs("h_second"), pairs("inv"), pairs("ccube")
         s, ex, g2, g3, tq, a, res = (pairs(n) for n in ("s", "ex", "gsq", "gcube", "tq", "a", "res"))
         rg = [s[1], s[0]]
-        q_col = tile("q_col", [P, U // P])
-
+        q_col = tile("q_col", [P, U // P])[:]
+        z_second[1] = z_second[0]
+        q_col = z_second[1][:, : U // P]
         quantise("r", 0, "S")
         quantise("r", 1, "V", 0, P)
         quantise("r", 1, "S", P, N)
@@ -180,8 +179,8 @@ def tile_picked_ygborn_force_p_kernel(
             nc.scalar.activation(lnb_win[b][:, :S], lnb[b], ACT.Ln, bias=1.0)
         for b in range(BLOCKS):
             nc.scalar.copy(y_win[b][:, :S], acc["y", b][:])
-        quantise("z", 0, "V")
-        quantise("z", 1, "V")
+        quantise("z", 0, "G")
+        quantise("z", 1, "G")
         product("z")
         for b in range(BLOCKS):
             nc.scalar.copy(z_win[b][:, :S], acc["z", b][:])
@@ -205,22 +204,23 @@ def tile_picked_ygborn_force_p_kernel(
             nc.scalar.activation(h_second[b], lnb_win[b][:].indirect(second[:]), ACT.Exp)
             turn(ln_ab[b], (h_first[b], h_second[b]))
         for b in range(BLOCKS):
-            nc.scalar.activation(dx2[b][:, :], dx[b][:, :], ACT.Square)
+            nc.vector.tensor_tensor(dx2[b][:, :], dx[b][:, :], dx[b][:, :], ALU.mult)
             nc.scalar.activation(inv[b], ln_ab[b], ACT.Exp, scale=-1.0, bias=2.0)
         for n, (b, lo, hi) in enumerate(pieces):
             nc.scalar.activation(dy2[b][:, lo:hi], dy[b][:, lo:hi], ACT.Square)
             rsq = bank(f"rsq{n}", ("x0", "x1", "z1")[n])
             turn(rsq, (dx2[b], dy2[b]), lo, hi)
             nc.vector.scalar_tensor_tensor(s[b][:, lo:hi], rsq[:, lo:hi], 0.1, inv[b][:, lo:hi], ALU.add, ALU.mult)
+        for b in range(BLOCKS):
+            nc.scalar.activation(c3[b], ln_ab[b], ACT.Exp, scale=-1.5, bias=3.0)
         for b, lo, hi in pieces:
             nc.scalar.activation(ex[b][:, lo:hi], s[b][:, lo:hi], ACT.Exp, scale=-0.25)
         q_turned = bank("q_turned", "z0")
         turn(q_turned, (q_pair,))
-        nc.vector.tensor_scalar(q_col[:], q_turned[:, 0:U:P], -0.25, None, ALU.mult)
+        nc.vector.tensor_scalar(q_col, q_turned[:, 0:U:P], -0.25, None, ALU.mult)
         dx_turned = [bank(f"dx_turned{b}", f"y{b}") for b in range(BLOCKS)]
         for b in range(BLOCKS):
             turn(dx_turned[b], (dx[b],))
-            nc.scalar.activation(c3[b], ln_ab[b], ACT.Exp, scale=-1.5, bias=3.0)
         g = [bank(f"g{b}", f"x{b}") for b in range(BLOCKS)]
         for b, lo, hi in pieces:
             turn(g[b], (s[b], ex[b]), lo, hi)

@@ -21,10 +21,15 @@ PACK = 4
 K_PASS = P * PACK
 PASSES = K // K_PASS
 BLOCKS = N // P
-VECTOR_WINDOW = 1024
-SCALAR_WINDOW = 2048
+QUADRANT = 32
+SCALE_ROWS = 4
+LIST_ROWS = 16
+RUN = 4
+POSITION_WINDOW = 1024
+RADIUS_WINDOW = 2048
 CHARGE_WINDOW = 704
 LN_FLOOR = 1e-19
+PIECES = [(0, 0, U), (1, 0, U // 2), (1, U // 2, U)]
 
 
 def tile_picked_ygborn_force_p_kernel(
@@ -38,20 +43,29 @@ def tile_picked_ygborn_force_p_kernel(
         def tile(name, shape, dtype=F32):
             return keep.tile(shape, dtype, name=name, align_bytes=64)
 
-        picked = tile("picked", [P, S // 16], U16)
-        first = tile("first", [P, U // 16], U16)
-        second = tile("second", [P, U // 16], U16)
+        def pairs(name):
+            return [tile(f"{name}{b}", [P, U])[:] for b in range(BLOCKS)]
+
+        def bank(name, tag):
+            return psum.tile([P, U], F32, name=name, tag=tag)[:]
+
+        picked = tile("picked", [P, S // LIST_ROWS], U16)
+        first = tile("first", [P, U // LIST_ROWS], U16)
+        second = tile("second", [P, U // LIST_ROWS], U16)
         words = [tile(f"words{o}", [P, T], U32) for o in range(PASSES)]
         scales = tile("scales", [P, T], U8)
         charge = tile("charge", [P, CHARGE_WINDOW])
-        y_win = [tile(f"y{b}", [P, VECTOR_WINDOW]) for b in range(BLOCKS)]
-        z_win = [tile(f"z{b}", [P, VECTOR_WINDOW]) for b in range(BLOCKS)]
-        lnb_win = [tile(f"lnb{b}", [P, SCALAR_WINDOW]) for b in range(BLOCKS)]
+        y_win = [tile(f"y_win{b}", [P, POSITION_WINDOW]) for b in range(BLOCKS)]
+        z_win = [tile(f"z_win{b}", [P, POSITION_WINDOW]) for b in range(BLOCKS)]
+        radius_win = [tile(f"radius_win{b}", [P, RADIUS_WINDOW]) for b in range(BLOCKS)]
         weights = {"r": w3, "y": w1, "z": w2}
         raw = {(m, o): tile(f"raw_{m}{o}", [P, PACK, N]) for m in weights for o in range(PASSES)}
-        sig = lnb_win[0][:, S : 3 * S]
         ln_sig = tile("ln_sig", [P, BLOCKS * S])[:]
         ident = tile("ident", [P, P])
+
+        sig = radius_win[0][:, S : 3 * S]
+        ln_born = [radius_win[1][:, (1 + b) * S : (2 + b) * S] for b in range(BLOCKS)]
+        softplus = [radius_win[b][:, 3 * S :] for b in range(BLOCKS)]
 
         nc.gpsimd.memset(scales[:].bitcast(I32), 0)
         nc.vector.memset(charge[:, S:], 0.0)
@@ -71,10 +85,10 @@ def tile_picked_ygborn_force_p_kernel(
 
         nc.sync.dma_start(out=picked[:], in_=offs)
         load_words(0)
-        for q in range(4):
+        for q in range(P // QUADRANT):
             nc.sync.dma_start(
-                out=scales[32 * q : 32 * q + 4 * PASSES, :].bitcast(I32),
-                in_=x_scales[:, 4 * q : 4 * q + 4, :].bitcast(I32),
+                out=scales[QUADRANT * q : QUADRANT * q + SCALE_ROWS * PASSES, :].bitcast(I32),
+                in_=x_scales[:, SCALE_ROWS * q : SCALE_ROWS * (q + 1), :].bitcast(I32),
             )
         load_weights("r", 0)
         load_words(1)
@@ -89,35 +103,26 @@ def tile_picked_ygborn_force_p_kernel(
 
         x_codes = [tile(f"x_codes{o}", [P, S], U32) for o in range(PASSES)]
         x_bytes = tile("x_bytes", [P, S], U8)
-        q_first = tile("q_first", [P, U])[:]
-        q_pair = tile("q_pair", [P, U])[:]
         nc.vector.tensor_copy(x_codes[0][:], words[0][:].indirect(picked[:]))
         nc.vector.tensor_copy(x_bytes[:], scales[:].indirect(picked[:]))
         nc.vector.tensor_copy(x_codes[1][:], words[1][:].indirect(picked[:]))
 
-        acc = {(m, b): psum.tile([P, S], F32, name=f"acc_{m}{b}", tag=f"{m}{b}") for m in weights for b in range(BLOCKS)}
-
+        acc = {(m, b): bank(f"acc_{m}{b}", f"{m}{b}") for m in weights for b in range(BLOCKS)}
         grouped = {key: tile(f"grouped_{key[0]}{key[1]}", [P, N * PACK], BF16)[:] for key in raw}
-        for o in (1,):
-            grouped["z", o] = ln_sig[:, o * S : (o + 1) * S].bitcast(BF16)
         codes = {key: tile(f"codes_{key[0]}{key[1]}", [P, N], U32) for key in raw}
         plane = {key: tile(f"plane_{key[0]}{key[1]}", [P, N], U8) for key in raw}
 
-        def quantise(m, o, engine, lo=0, hi=N):
-            dst = grouped[m, o][:, lo * PACK : hi * PACK].rearrange("p (c i t) -> p c t i", i=4, t=PACK)
-            src = raw[m, o][:, :, lo:hi].rearrange("p t (c i) -> p c t i", i=4)
-            if engine == "S":
-                nc.scalar.copy(dst, src)
-            elif engine == "V":
-                nc.vector.tensor_copy(dst, src)
-            else:
-                nc.gpsimd.tensor_scalar(
-                    grouped[m, o].rearrange("p (n t) -> p n t", t=PACK), raw[m, o][:].rearrange("p t n -> p n t"), 1.0, 0.0, ALU.mult, ALU.add
-                )
+        def gpsimd_round(dst, src):
+            nc.gpsimd.tensor_scalar(dst, src, 1.0, 0.0, ALU.mult, ALU.add)
+
+        def quantise(m, o, rounding, run, lo=0, hi=N):
+            values = grouped[m, o][:, lo * PACK : hi * PACK]
+            rounding(
+                values.rearrange("p (c i t) -> p c t i", i=run, t=PACK),
+                raw[m, o][:, :, lo:hi].rearrange("p t (c i) -> p c t i", i=run),
+            )
             nc.vector.quantize_mx(
-                out=codes[m, o][:, lo:hi].bitcast(FP8X4),
-                scales=plane[m, o][:, lo:hi],
-                in_=grouped[m, o][:, lo * PACK : hi * PACK],
+                out=codes[m, o][:, lo:hi].bitcast(FP8X4), scales=plane[m, o][:, lo:hi], in_=values
             )
 
         def product(m):
@@ -125,117 +130,132 @@ def tile_picked_ygborn_force_p_kernel(
                 cols = slice(b * P, (b + 1) * P)
                 for o in range(PASSES):
                     nc.tensor.matmul_mx(
-                        out=acc[m, b][:],
+                        out=acc[m, b],
                         lhsT=codes[m, o][:, cols].bitcast(FP8X4),
                         lhsT_scale=plane[m, o][:, cols],
                         rhs=x_codes[o][:].bitcast(FP8X4),
-                        rhs_scale=x_bytes[4 * o :, :],
+                        rhs_scale=x_bytes[SCALE_ROWS * o :, :],
                         start=(o == 0),
                         stop=(o == PASSES - 1),
                     )
 
-        def pairs(name):
-            return [tile(f"{name}{b}", [P, U])[:] for b in range(BLOCKS)]
-
-        def turn(bank, terms, lo=0, hi=U):
+        def turn(target, terms, lo=0, hi=U):
             for j in range(lo // P, hi // P):
                 cols = slice(j * P, (j + 1) * P)
                 for n, term in enumerate(terms):
                     nc.tensor.matmul(
-                        bank[:, cols], term[:, cols], ident[:], is_transpose=True,
-                        start=(n == 0), stop=(n == len(terms) - 1),
+                        target[:, cols],
+                        term[:, cols],
+                        ident[:],
+                        is_transpose=True,
+                        start=(n == 0),
+                        stop=(n == len(terms) - 1),
                     )
 
-        def bank(name, tag):
-            return psum.tile([P, U], F32, name=name, tag=tag)[:]
+        q_first, q_pair = tile("q_first", [P, U])[:], tile("q_pair", [P, U])[:]
+        dx, dy, dx_sq, dy_sq = pairs("dx"), pairs("dy"), pairs("dx_sq"), pairs("dy_sq")
+        lb_first, lb_second = pairs("lb_first"), pairs("lb_second")
+        inv_ab, ab_power, s, ex = pairs("inv_ab"), pairs("ab_power"), pairs("s"), pairs("ex")
+        pull, factor, root_sq, partial, result = (
+            pairs(name) for name in ("pull", "factor", "root_sq", "partial", "result")
+        )
+        y_second = [tile("y_second", [P, U])[:], grouped["z", 1].bitcast(F32)]
+        z_second = tile("z_second", [P, U])[:]
+        q_col = z_second[:, : U // P]
+        root = [s[1], s[0]]
 
-        y_second, dx, z_second, dy = pairs("y_second"), pairs("dx"), pairs("z_second"), pairs("dy")
-        dx2, dy2 = pairs("dx2"), pairs("dy2")
-        soft = [lnb_win[b][:, 3 * S :] for b in range(BLOCKS)]
-        lnb = [lnb_win[1][:, (1 + b) * S : (2 + b) * S] for b in range(BLOCKS)]
-        h_first, h_second, inv, c3 = pairs("h_first"), pairs("h_second"), pairs("inv"), pairs("ccube")
-        s, ex, g2, g3, tq, a, res = (pairs(n) for n in ("s", "ex", "gsq", "gcube", "tq", "a", "res"))
-        rg = [s[1], s[0]]
-        q_col = tile("q_col", [P, U // P])[:]
-        z_second[1] = z_second[0]
-        q_col = z_second[1][:, : U // P]
-        quantise("r", 0, "S")
-        quantise("r", 1, "V", 0, P)
-        quantise("r", 1, "S", P, N)
+        quantise("r", 0, nc.scalar.copy, RUN)
+        quantise("r", 1, nc.vector.tensor_copy, RUN, 0, P)
+        quantise("r", 1, nc.scalar.copy, RUN, P, N)
         product("r")
-        quantise("y", 0, "V")
-        quantise("y", 1, "V")
+        quantise("y", 0, gpsimd_round, 1)
+        quantise("y", 1, nc.vector.tensor_copy, RUN)
         product("y")
+
         for b in range(BLOCKS):
-            nc.scalar.activation(sig[:, b * S : (b + 1) * S], acc["r", b][:], ACT.Sigmoid, scale=-1.0)
+            nc.scalar.activation(sig[:, b * S : (b + 1) * S], acc["r", b], ACT.Sigmoid, scale=-1.0)
         nc.scalar.activation(ln_sig, sig, ACT.Ln, bias=LN_FLOOR)
         for b in range(BLOCKS):
             nc.vector.scalar_tensor_tensor(
-                soft[b], ln_sig[:, b * S : (b + 1) * S], -1.0, acc["r", b][:], ALU.mult, ALU.max
+                softplus[b], ln_sig[:, b * S : (b + 1) * S], -1.0, acc["r", b], ALU.mult, ALU.max
             )
         for b in range(BLOCKS):
-            nc.scalar.activation(lnb[b], soft[b], ACT.Ln, bias=0.4)
+            nc.scalar.activation(ln_born[b], softplus[b], ACT.Ln, bias=0.4)
         for b in range(BLOCKS):
-            nc.scalar.activation(lnb_win[b][:, :S], lnb[b], ACT.Ln, bias=1.0)
+            nc.scalar.activation(radius_win[b][:, :S], ln_born[b], ACT.Ln, bias=1.0)
+
         for b in range(BLOCKS):
-            nc.scalar.copy(y_win[b][:, :S], acc["y", b][:])
-        quantise("z", 0, "G")
-        quantise("z", 1, "G")
+            nc.scalar.copy(y_win[b][:, :S], acc["y", b])
+        quantise("z", 0, gpsimd_round, 1)
+        quantise("z", 1, gpsimd_round, 1)
         product("z")
         for b in range(BLOCKS):
-            nc.scalar.copy(z_win[b][:, :S], acc["z", b][:])
-        pieces = [(0, 0, U), (1, 0, U // 2), (1, U // 2, U)]
-        tail = [(0, 0, U), (1, 0, U // 2), (1, U // 2, U)]
+            nc.scalar.copy(z_win[b][:, :S], acc["z", b])
+
         for b in range(BLOCKS):
             nc.vector.tensor_copy(y_second[b], y_win[b][:].indirect(second[:]))
             nc.vector.tensor_tensor(dx[b], y_win[b][:].indirect(first[:]), y_second[b], ALU.subtract)
-        for b in range(BLOCKS):
-            nc.vector.tensor_copy(z_second[b], z_win[b][:].indirect(second[:]))
-            for c, lo, hi in pieces:
-                if c == b:
-                    nc.vector.tensor_tensor(
-                        dy[b][:, lo:hi], z_win[b][:].indirect(first[:, lo // 16 : hi // 16]), z_second[b][:, lo:hi], ALU.subtract
-                    )
+        for b, lo, hi in PIECES:
+            if lo == 0:
+                nc.vector.tensor_copy(z_second, z_win[b][:].indirect(second[:]))
+            nc.vector.tensor_tensor(
+                dy[b][:, lo:hi],
+                z_win[b][:].indirect(first[:, lo // LIST_ROWS : hi // LIST_ROWS]),
+                z_second[:, lo:hi],
+                ALU.subtract,
+            )
         nc.vector.tensor_copy(q_first, charge[:].indirect(first[:]))
         nc.vector.tensor_tensor(q_pair, charge[:].indirect(second[:]), q_first, ALU.mult)
-        ln_ab = [bank(f"ln_ab{b}", f"r{b}") for b in range(BLOCKS)]
+
+        ln_ab2 = [bank(f"ln_ab2_{b}", f"r{b}") for b in range(BLOCKS)]
         for b in range(BLOCKS):
-            nc.scalar.activation(h_first[b], lnb_win[b][:].indirect(first[:]), ACT.Exp)
-            nc.scalar.activation(h_second[b], lnb_win[b][:].indirect(second[:]), ACT.Exp)
-            turn(ln_ab[b], (h_first[b], h_second[b]))
+            nc.scalar.activation(lb_first[b], radius_win[b][:].indirect(first[:]), ACT.Exp)
+            nc.scalar.activation(lb_second[b], radius_win[b][:].indirect(second[:]), ACT.Exp)
+            turn(ln_ab2[b], (lb_first[b], lb_second[b]))
+
         for b in range(BLOCKS):
-            nc.vector.tensor_tensor(dx2[b][:, :], dx[b][:, :], dx[b][:, :], ALU.mult)
-            nc.scalar.activation(inv[b], ln_ab[b], ACT.Exp, scale=-1.0, bias=2.0)
-        for n, (b, lo, hi) in enumerate(pieces):
-            nc.scalar.activation(dy2[b][:, lo:hi], dy[b][:, lo:hi], ACT.Square)
-            rsq = bank(f"rsq{n}", ("x0", "x1", "z1")[n])
-            turn(rsq, (dx2[b], dy2[b]), lo, hi)
-            nc.vector.scalar_tensor_tensor(s[b][:, lo:hi], rsq[:, lo:hi], 0.1, inv[b][:, lo:hi], ALU.add, ALU.mult)
+            nc.scalar.activation(dx_sq[b], dx[b], ACT.Square)
+            nc.scalar.activation(inv_ab[b], ln_ab2[b], ACT.Exp, scale=-1.0, bias=2.0)
+        for (b, lo, hi), tag in zip(PIECES, ("x0", "x1", "z1")):
+            nc.vector.tensor_tensor(dy_sq[b][:, lo:hi], dy[b][:, lo:hi], dy[b][:, lo:hi], ALU.mult)
+            squares = bank(f"squares_{tag}", tag)
+            turn(squares, (dx_sq[b], dy_sq[b]), lo, hi)
+            nc.vector.scalar_tensor_tensor(
+                s[b][:, lo:hi], squares[:, lo:hi], 0.1, inv_ab[b][:, lo:hi], ALU.add, ALU.mult
+            )
         for b in range(BLOCKS):
-            nc.scalar.activation(c3[b], ln_ab[b], ACT.Exp, scale=-1.5, bias=3.0)
-        for b, lo, hi in pieces:
+            nc.scalar.activation(ab_power[b], ln_ab2[b], ACT.Exp, scale=-1.5, bias=3.0)
+        for b, lo, hi in PIECES:
             nc.scalar.activation(ex[b][:, lo:hi], s[b][:, lo:hi], ACT.Exp, scale=-0.25)
+
         q_turned = bank("q_turned", "z0")
         turn(q_turned, (q_pair,))
         nc.vector.tensor_scalar(q_col, q_turned[:, 0:U:P], -0.25, None, ALU.mult)
         dx_turned = [bank(f"dx_turned{b}", f"y{b}") for b in range(BLOCKS)]
         for b in range(BLOCKS):
             turn(dx_turned[b], (dx[b],))
+
         g = [bank(f"g{b}", f"x{b}") for b in range(BLOCKS)]
-        for b, lo, hi in pieces:
+        for b, lo, hi in PIECES:
             turn(g[b], (s[b], ex[b]), lo, hi)
-        a_back = [bank(f"a_back{b}", f"z{b}") for b in range(BLOCKS)]
+        factor_plain = [bank(f"factor_plain{b}", f"z{b}") for b in range(BLOCKS)]
         for b in range(BLOCKS):
             for j in range(U // P):
                 cols = slice(j * P, (j + 1) * P)
                 nc.vector.scalar_tensor_tensor(
-                    tq[b][:, cols], dx_turned[b][:, cols], q_col[:, j : j + 1], c3[b][:, cols], ALU.mult, ALU.mult
+                    pull[b][:, cols],
+                    dx_turned[b][:, cols],
+                    q_col[:, j : j + 1],
+                    ab_power[b][:, cols],
+                    ALU.mult,
+                    ALU.mult,
                 )
-            nc.vector.scalar_tensor_tensor(a[b], ex[b], -4.0, tq[b], ALU.add, ALU.mult)
-            turn(a_back[b], (a[b],))
-        for b, lo, hi in tail:
-            nc.scalar.activation(rg[b][:, lo:hi], g[b][:, lo:hi], ACT.Abs_reciprocal_sqrt)
-            nc.scalar.activation(g2[b][:, lo:hi], rg[b][:, lo:hi], ACT.Square)
-            nc.vector.tensor_tensor(g3[b][:, lo:hi], a_back[b][:, lo:hi], rg[b][:, lo:hi], ALU.mult)
-            nc.vector.tensor_tensor(res[b][:, lo:hi], g3[b][:, lo:hi], g2[b][:, lo:hi], ALU.mult)
-            nc.sync.dma_start(out=out[b * P : (b + 1) * P, lo:hi], in_=res[b][:, lo:hi])
+            nc.vector.scalar_tensor_tensor(factor[b], ex[b], -4.0, pull[b], ALU.add, ALU.mult)
+            turn(factor_plain[b], (factor[b],))
+
+        for b, lo, hi in PIECES:
+            nc.scalar.activation(root[b][:, lo:hi], g[b][:, lo:hi], ACT.Abs_reciprocal_sqrt)
+            nc.scalar.activation(root_sq[b][:, lo:hi], root[b][:, lo:hi], ACT.Square)
+            nc.vector.tensor_tensor(partial[b][:, lo:hi], factor_plain[b][:, lo:hi], root[b][:, lo:hi], ALU.mult)
+            nc.vector.tensor_tensor(result[b][:, lo:hi], partial[b][:, lo:hi], root_sq[b][:, lo:hi], ALU.mult)
+            nc.sync.dma_start(out=out[b * P : (b + 1) * P, lo:hi], in_=result[b][:, lo:hi])

from contextlib import ExitStack

import concourse.mybir as mybir
from concourse.masks import make_identity

K, T, S, N, U = 1024, 1024, 512, 256, 512
FLOPS = 3 * 2 * K * N * S

F32 = mybir.dt.float32
BF16 = mybir.dt.bfloat16
I32 = mybir.dt.int32
U32 = mybir.dt.uint32
U16 = mybir.dt.uint16
U8 = mybir.dt.uint8
FP8X4 = mybir.dt.float8_e4m3fn_x4
ALU = mybir.AluOpType
ACT = mybir.ActivationFunctionType

P = 128
PACK = 4
K_PASS = P * PACK
PASSES = K // K_PASS
BLOCKS = N // P
QUADRANT = 32
SCALE_ROWS = 4
LIST_ROWS = 16
RUN = 4
POSITION_WINDOW = 1024
RADIUS_WINDOW = 2048
CHARGE_WINDOW = 704
LN_FLOOR = 1e-19
PIECES = [(0, 0, U), (1, 0, U // 2), (1, U // 2, U)]


def tile_picked_ygborn_force_p_kernel(
    tc, x_words, x_scales, w1, w2, w3, chg, offs, ia, ib, out
):
    nc = tc.nc
    with ExitStack() as ctx:
        keep = ctx.enter_context(tc.tile_pool(name="keep", bufs=1))
        psum = ctx.enter_context(tc.psum_pool(name="psum", bufs=1))

        def tile(name, shape, dtype=F32):
            return keep.tile(shape, dtype, name=name, align_bytes=64)

        def pairs(name):
            return [tile(f"{name}{b}", [P, U])[:] for b in range(BLOCKS)]

        def bank(name, tag):
            return psum.tile([P, U], F32, name=name, tag=tag)[:]

        picked = tile("picked", [P, S // LIST_ROWS], U16)
        first = tile("first", [P, U // LIST_ROWS], U16)
        second = tile("second", [P, U // LIST_ROWS], U16)
        words = [tile(f"words{o}", [P, T], U32) for o in range(PASSES)]
        scales = tile("scales", [P, T], U8)
        charge = tile("charge", [P, CHARGE_WINDOW])
        y_win = [tile(f"y_win{b}", [P, POSITION_WINDOW]) for b in range(BLOCKS)]
        z_win = [tile(f"z_win{b}", [P, POSITION_WINDOW]) for b in range(BLOCKS)]
        radius_win = [tile(f"radius_win{b}", [P, RADIUS_WINDOW]) for b in range(BLOCKS)]
        weights = {"r": w3, "y": w1, "z": w2}
        raw = {(m, o): tile(f"raw_{m}{o}", [P, PACK, N]) for m in weights for o in range(PASSES)}
        ln_sig = tile("ln_sig", [P, BLOCKS * S])[:]
        ident = tile("ident", [P, P])

        sig = radius_win[0][:, S : 3 * S]
        ln_born = [radius_win[1][:, (1 + b) * S : (2 + b) * S] for b in range(BLOCKS)]
        softplus = [radius_win[b][:, 3 * S :] for b in range(BLOCKS)]

        nc.gpsimd.memset(scales[:].bitcast(I32), 0)
        nc.vector.memset(charge[:, S:], 0.0)
        for win in y_win + z_win:
            nc.vector.memset(win[:, S:], 0.0)
        make_identity(nc, ident[:])

        def load_weights(m, o):
            rows = weights[m][o * K_PASS : (o + 1) * K_PASS, :]
            nc.sync.dma_start(out=raw[m, o][:], in_=rows.rearrange("(p j) n -> p j n", j=PACK))

        def load_words(o):
            nc.sync.dma_start(
                out=words[o][:].bitcast(I32),
                in_=x_words[o].rearrange("p n t -> p (n t)").bitcast(I32),
            )

        nc.sync.dma_start(out=picked[:], in_=offs)
        load_words(0)
        for q in range(P // QUADRANT):
            nc.sync.dma_start(
                out=scales[QUADRANT * q : QUADRANT * q + SCALE_ROWS * PASSES, :].bitcast(I32),
                in_=x_scales[:, SCALE_ROWS * q : SCALE_ROWS * (q + 1), :].bitcast(I32),
            )
        load_weights("r", 0)
        load_words(1)
        load_weights("r", 1)
        load_weights("y", 0)
        load_weights("y", 1)
        nc.sync.dma_start(out=first[:], in_=ia)
        nc.sync.dma_start(out=second[:], in_=ib)
        nc.sync.dma_start(out=charge[:, :S], in_=chg)
        load_weights("z", 0)
        load_weights("z", 1)

        x_codes = [tile(f"x_codes{o}", [P, S], U32) for o in range(PASSES)]
        x_bytes = tile("x_bytes", [P, S], U8)
        nc.vector.tensor_copy(x_codes[0][:], words[0][:].indirect(picked[:]))
        nc.vector.tensor_copy(x_bytes[:], scales[:].indirect(picked[:]))
        nc.vector.tensor_copy(x_codes[1][:], words[1][:].indirect(picked[:]))

        acc = {(m, b): bank(f"acc_{m}{b}", f"{m}{b}") for m in weights for b in range(BLOCKS)}
        grouped = {key: tile(f"grouped_{key[0]}{key[1]}", [P, N * PACK], BF16)[:] for key in raw}
        codes = {key: tile(f"codes_{key[0]}{key[1]}", [P, N], U32) for key in raw}
        plane = {key: tile(f"plane_{key[0]}{key[1]}", [P, N], U8) for key in raw}

        def gpsimd_round(dst, src):
            nc.gpsimd.tensor_scalar(dst, src, 1.0, 0.0, ALU.mult, ALU.add)

        def quantise(m, o, rounding, run, lo=0, hi=N):
            values = grouped[m, o][:, lo * PACK : hi * PACK]
            rounding(
                values.rearrange("p (c i t) -> p c t i", i=run, t=PACK),
                raw[m, o][:, :, lo:hi].rearrange("p t (c i) -> p c t i", i=run),
            )
            nc.vector.quantize_mx(
                out=codes[m, o][:, lo:hi].bitcast(FP8X4), scales=plane[m, o][:, lo:hi], in_=values
            )

        def product(m):
            for b in range(BLOCKS):
                cols = slice(b * P, (b + 1) * P)
                for o in range(PASSES):
                    nc.tensor.matmul_mx(
                        out=acc[m, b],
                        lhsT=codes[m, o][:, cols].bitcast(FP8X4),
                        lhsT_scale=plane[m, o][:, cols],
                        rhs=x_codes[o][:].bitcast(FP8X4),
                        rhs_scale=x_bytes[SCALE_ROWS * o :, :],
                        start=(o == 0),
                        stop=(o == PASSES - 1),
                    )

        def turn(target, terms, lo=0, hi=U):
            for j in range(lo // P, hi // P):
                cols = slice(j * P, (j + 1) * P)
                for n, term in enumerate(terms):
                    nc.tensor.matmul(
                        target[:, cols],
                        term[:, cols],
                        ident[:],
                        is_transpose=True,
                        start=(n == 0),
                        stop=(n == len(terms) - 1),
                    )

        q_first, q_pair = tile("q_first", [P, U])[:], tile("q_pair", [P, U])[:]
        dx, dy, dx_sq, dy_sq = pairs("dx"), pairs("dy"), pairs("dx_sq"), pairs("dy_sq")
        lb_first, lb_second = pairs("lb_first"), pairs("lb_second")
        inv_ab, ab_power, s, ex = pairs("inv_ab"), pairs("ab_power"), pairs("s"), pairs("ex")
        pull, factor, root_sq, partial, result = (
            pairs(name) for name in ("pull", "factor", "root_sq", "partial", "result")
        )
        y_second = [tile("y_second", [P, U])[:], grouped["z", 1].bitcast(F32)]
        z_second = tile("z_second", [P, U])[:]
        q_col = z_second[:, : U // P]
        root = [s[1], s[0]]

        quantise("r", 0, nc.scalar.copy, RUN)
        quantise("r", 1, nc.vector.tensor_copy, RUN, 0, P)
        quantise("r", 1, nc.scalar.copy, RUN, P, N)
        product("r")
        quantise("y", 0, gpsimd_round, 1)
        quantise("y", 1, nc.vector.tensor_copy, RUN)
        product("y")

        for b in range(BLOCKS):
            nc.scalar.activation(sig[:, b * S : (b + 1) * S], acc["r", b], ACT.Sigmoid, scale=-1.0)
        nc.scalar.activation(ln_sig, sig, ACT.Ln, bias=LN_FLOOR)
        for b in range(BLOCKS):
            nc.vector.scalar_tensor_tensor(
                softplus[b], ln_sig[:, b * S : (b + 1) * S], -1.0, acc["r", b], ALU.mult, ALU.max
            )
        for b in range(BLOCKS):
            nc.scalar.activation(ln_born[b], softplus[b], ACT.Ln, bias=0.4)
        for b in range(BLOCKS):
            nc.scalar.activation(radius_win[b][:, :S], ln_born[b], ACT.Ln, bias=1.0)

        for b in range(BLOCKS):
            nc.scalar.copy(y_win[b][:, :S], acc["y", b])
        quantise("z", 0, gpsimd_round, 1)
        quantise("z", 1, gpsimd_round, 1)
        product("z")
        for b in range(BLOCKS):
            nc.scalar.copy(z_win[b][:, :S], acc["z", b])

        for b in range(BLOCKS):
            nc.vector.tensor_copy(y_second[b], y_win[b][:].indirect(second[:]))
            nc.vector.tensor_tensor(dx[b], y_win[b][:].indirect(first[:]), y_second[b], ALU.subtract)
        for b, lo, hi in PIECES:
            if lo == 0:
                nc.vector.tensor_copy(z_second, z_win[b][:].indirect(second[:]))
            nc.vector.tensor_tensor(
                dy[b][:, lo:hi],
                z_win[b][:].indirect(first[:, lo // LIST_ROWS : hi // LIST_ROWS]),
                z_second[:, lo:hi],
                ALU.subtract,
            )
        nc.vector.tensor_copy(q_first, charge[:].indirect(first[:]))
        nc.vector.tensor_tensor(q_pair, charge[:].indirect(second[:]), q_first, ALU.mult)

        ln_ab2 = [bank(f"ln_ab2_{b}", f"r{b}") for b in range(BLOCKS)]
        for b in range(BLOCKS):
            nc.scalar.activation(lb_first[b], radius_win[b][:].indirect(first[:]), ACT.Exp)
            nc.scalar.activation(lb_second[b], radius_win[b][:].indirect(second[:]), ACT.Exp)
            turn(ln_ab2[b], (lb_first[b], lb_second[b]))

        for b in range(BLOCKS):
            nc.scalar.activation(dx_sq[b], dx[b], ACT.Square)
            nc.scalar.activation(inv_ab[b], ln_ab2[b], ACT.Exp, scale=-1.0, bias=2.0)
        for (b, lo, hi), tag in zip(PIECES, ("x0", "x1", "z1")):
            nc.vector.tensor_tensor(dy_sq[b][:, lo:hi], dy[b][:, lo:hi], dy[b][:, lo:hi], ALU.mult)
            squares = bank(f"squares_{tag}", tag)
            turn(squares, (dx_sq[b], dy_sq[b]), lo, hi)
            nc.vector.scalar_tensor_tensor(
                s[b][:, lo:hi], squares[:, lo:hi], 0.1, inv_ab[b][:, lo:hi], ALU.add, ALU.mult
            )
        for b in range(BLOCKS):
            nc.scalar.activation(ab_power[b], ln_ab2[b], ACT.Exp, scale=-1.5, bias=3.0)
        for b, lo, hi in PIECES:
            nc.scalar.activation(ex[b][:, lo:hi], s[b][:, lo:hi], ACT.Exp, scale=-0.25)

        q_turned = bank("q_turned", "z0")
        turn(q_turned, (q_pair,))
        nc.vector.tensor_scalar(q_col, q_turned[:, 0:U:P], -0.25, None, ALU.mult)
        dx_turned = [bank(f"dx_turned{b}", f"y{b}") for b in range(BLOCKS)]
        for b in range(BLOCKS):
            turn(dx_turned[b], (dx[b],))

        g = [bank(f"g{b}", f"x{b}") for b in range(BLOCKS)]
        for b, lo, hi in PIECES:
            turn(g[b], (s[b], ex[b]), lo, hi)
        factor_plain = [bank(f"factor_plain{b}", f"z{b}") for b in range(BLOCKS)]
        for b in range(BLOCKS):
            for j in range(U // P):
                cols = slice(j * P, (j + 1) * P)
                nc.vector.scalar_tensor_tensor(
                    pull[b][:, cols],
                    dx_turned[b][:, cols],
                    q_col[:, j : j + 1],
                    ab_power[b][:, cols],
                    ALU.mult,
                    ALU.mult,
                )
            nc.vector.scalar_tensor_tensor(factor[b], ex[b], -4.0, pull[b], ALU.add, ALU.mult)
            turn(factor_plain[b], (factor[b],))

        for b, lo, hi in PIECES:
            nc.scalar.activation(root[b][:, lo:hi], g[b][:, lo:hi], ACT.Abs_reciprocal_sqrt)
            nc.scalar.activation(root_sq[b][:, lo:hi], root[b][:, lo:hi], ACT.Square)
            nc.vector.tensor_tensor(partial[b][:, lo:hi], factor_plain[b][:, lo:hi], root[b][:, lo:hi], ALU.mult)
            nc.vector.tensor_tensor(result[b][:, lo:hi], partial[b][:, lo:hi], root_sq[b][:, lo:hi], ALU.mult)
            nc.sync.dma_start(out=out[b * P : (b + 1) * P, lo:hi], in_=result[b][:, lo:hi])
